import numpy as np
import ml_dtypes


def mxq(x, axis, fmt="e4m3"):
    dtype, down = {"e4m3": (ml_dtypes.float8_e4m3fn, 7), "e5m2": (ml_dtypes.float8_e5m2, 14)}[fmt]
    v = np.moveaxis(np.asarray(x, np.float32).astype(ml_dtypes.bfloat16).astype(np.float64), axis, -1)
    blocks = v.reshape(v.shape[:-1] + (-1, 32))
    amax = np.abs(blocks).max(-1, keepdims=True)
    byte = np.maximum(np.where(amax > 0, np.frexp(amax)[1] - 1 + 127, 0) - down, 1)
    scale = np.exp2(byte - 127.0)
    codes = (blocks / scale).astype(np.float32).astype(dtype).astype(np.float64)
    return np.moveaxis((codes * scale).reshape(v.shape), -1, axis)


WIDE = False


def mx_kscale(k):
    if not WIDE:
        return np.ones(k)
    levels = np.array([30, -30])
    if k % 512:
        return np.exp2(np.random.permutation(np.resize(levels, k // 32))).repeat(32)
    a = np.empty((k // 512, 16))
    for p in range(k // 512):
        a[p, :8] = np.random.permutation(np.resize(levels, 8))
        for g in range(8):
            far = levels[np.abs(levels - a[p, g]) >= 10]
            a[p, g + 8] = far[np.random.randint(len(far))]
    return np.exp2(a.ravel()).repeat(32)


BF16 = ml_dtypes.bfloat16


def bf(x):
    return np.asarray(x, np.float32).astype(BF16)


def f64(x):
    return np.asarray(x).astype(np.float64)


E2M1 = np.array([0.0, 0.5, 1.0, 1.5, 2.0, 3.0, 4.0, 6.0, -0.0, -0.5, -1.0, -1.5, -2.0, -3.0, -4.0, -6.0])


def pack_weight(w, fmt):
    k, n = w.shape
    w = f64(bf(w)).reshape(k // 32, 32, n)
    amax = np.abs(w).max(1)
    if fmt in ("e4m3", "e5m2"):
        byte = np.frexp(amax)[1] - 1 + 127 - (7 if fmt == "e4m3" else 14)
    else:
        mant, ex = np.frexp(amax / 6.0)
        byte = np.where(mant > 0.5, ex, ex - 1) + 127
    byte = np.clip(np.where(amax > 0, byte, 1), 1, 254)
    scaled = (w * np.exp2(127.0 - byte)[:, None, :]).reshape(k, n).astype(np.float32)
    by_word = np.ascontiguousarray(scaled.reshape(k // 512, 128, 4, n).transpose(0, 1, 3, 2))
    if fmt in ("e4m3", "e5m2"):
        words = by_word.astype(ml_dtypes.float8_e4m3fn if fmt == "e4m3" else ml_dtypes.float8_e5m2).view(np.uint8)
    else:
        c = by_word.astype(ml_dtypes.float4_e2m1fn).view(np.uint8) & 0xF
        words = c[..., 0::2] | (c[..., 1::2] << 4)
    return np.ascontiguousarray(words), np.ascontiguousarray(byte.astype(np.uint8).reshape(k // 512, 16, n))


def unpack_weight(words, scales, fmt):
    g, p, n, _ = words.shape
    if fmt in ("e4m3", "e5m2"):
        vals = np.ascontiguousarray(words).view(ml_dtypes.float8_e4m3fn if fmt == "e4m3" else ml_dtypes.float8_e5m2).astype(np.float64)
    else:
        nib = np.empty((g, p, n, 4), np.uint8)
        nib[..., 0::2] = words & 0xF
        nib[..., 1::2] = words >> 4
        vals = E2M1[nib]
    vals = vals * np.repeat(np.exp2(scales.astype(np.float64) - 127.0), 8, axis=1)[..., None]
    return vals.transpose(0, 1, 3, 2).reshape(g * 512, n)

def planes(Y):
    n, m = Y.shape
    b = f64(bf(Y)).reshape(n // 32, 32, m)
    amax = np.abs(b).max(1)
    byte = np.clip(np.where(amax > 0, np.frexp(amax)[1] - 1 + 127 - 7, 1), 1, 254)
    codes = (b * np.exp2(127.0 - byte)[:, None, :]).reshape(n, m).astype(np.float32).astype(ml_dtypes.float8_e4m3fn).view(np.uint8)
    words = codes.reshape(n // 512, 128, 4, m).transpose(0, 1, 3, 2)
    return np.ascontiguousarray(words), np.ascontiguousarray(byte.astype(np.uint8).reshape(n // 512, 16, m))


M, N, K = 1536, 2048, 1024


def setup_inputs():
    s = mx_kscale(K)
    size = np.exp(0.8 * np.random.randn(N))
    A = np.random.randn(M, N) * np.exp(0.6 * np.random.randn(M, N) - 0.36) * size
    cols = np.random.permutation(N)[:K]
    rows = np.random.permutation(M)[:K]
    C = A[:, cols] / size[cols] * s
    core = (0.7 + 0.15 * np.random.randn(K)) / np.sqrt(K) / s
    c_words, c_scales = pack_weight(C.T, "e5m2")
    row_weight = np.exp(0.3 * np.random.randn(M))
    return {"a": bf(A), "c_words": c_words, "c_scales": c_scales, "core": bf(core),
            "r": bf(A[rows, :]), "row_weight": bf(row_weight)}

def reference(a, c_words, c_scales, core, r, row_weight):
    C = unpack_weight(c_words, c_scales, "e5m2").T
    UR = mxq(f64(core)[:, None] * f64(r), 0, "e4m3")
    approx = C @ UR
    y = (f64(a) - approx) * f64(row_weight)[:, None]
    Y = y.T
    words, scales = planes(Y)
    return y, words, scales

@@ -1,0 +1,296 @@
+from contextlib import ExitStack
+
+import concourse.mybir as mybir
+from concourse.masks import make_identity
+
+M, N, K = 1536, 2048, 1024
+FLOPS = 2 * M * N * K
+
+F32 = mybir.dt.float32
+BF16 = mybir.dt.bfloat16
+I32 = mybir.dt.int32
+U32 = mybir.dt.uint32
+U8 = mybir.dt.uint8
+E4M3X4 = mybir.dt.float8_e4m3fn_x4
+E5M2X4 = mybir.dt.float8_e5m2_x4
+MULT = mybir.AluOpType.mult
+ADD = mybir.AluOpType.add
+COPY = mybir.ActivationFunctionType.Copy
+
+P = 128
+PACK = 4
+GROUP = P * PACK
+PASSES = K // GROUP
+GROUPS = N // GROUP
+TILES = 4
+BANDS = M // (TILES * P)
+UNITS = GROUPS * BANDS
+HALF = GROUP // 2
+RUN = 288
+SHARED_FROM = 7
+
+
+def tile_cur_residual_planes_k2_kernel(tc, a, c_words, c_scales, core, r, row_weight, out_0, out_1, out_2):
+    nc = tc.nc
+    with ExitStack() as ctx:
+        keep = ctx.enter_context(tc.tile_pool(name="keep", bufs=1))
+        ypool = ctx.enter_context(tc.tile_pool(name="ypool", bufs=8))
+        ring = ctx.enter_context(tc.tile_pool(name="ring", bufs=2))
+        opool = ctx.enter_context(tc.tile_pool(name="opool", bufs=8))
+        accs = ctx.enter_context(tc.psum_pool(name="accs", bufs=TILES))
+        turns = ctx.enter_context(tc.psum_pool(name="turns", bufs=4))
+        ctx.enter_context(tc.manual_schedule())
+
+        ident = keep.tile([P, P], F32, name="ident")
+        make_identity(nc, ident[:])
+        c_plane = keep.tile([P, PASSES, M], U8, name="c_plane", align_bytes=64)
+        w_rows = keep.tile([P, P], BF16, name="w_rows")
+        nc.vector.memset(w_rows[:], 0.0)
+        nc.vector.memset(c_plane[:].rearrange("p c m -> p (c m)").bitcast(I32), 0)
+
+        core_bf = keep.tile([P, PASSES, PACK], BF16, name="core_bf")
+        nc.scalar.dma_start(out=core_bf[:], in_=core.rearrange("(c p t) -> p c t", c=PASSES, t=PACK))
+        w_src = row_weight.rearrange("(j p) -> j p", p=P)
+        nc.scalar.dma_start(out=w_rows[:8, :], in_=w_src[:8, :])
+        nc.scalar.dma_start(out=w_rows[8 : M // P, :], in_=w_src[8:, :])
+        core_sb = keep.tile([P, PASSES, PACK], F32, name="core_sb")
+        nc.scalar.activation(out=core_sb[:], in_=core_bf[:], func=COPY)
+
+        r_sb = {}
+        a_sb = {}
+        c_sb = {}
+
+        def load_r(g):
+            for c in range(PASSES):
+                t = keep.tile([P, PACK, GROUP], BF16, name="r_%d_%d" % (g, c), align_bytes=64)
+                src = r[c * GROUP : (c + 1) * GROUP, g * GROUP : (g + 1) * GROUP]
+                nc.sync.dma_start(out=t[:], in_=src.rearrange("(p t) n -> p t n", t=PACK))
+                r_sb[(g, c)] = t
+
+        def load_a(g, b0, b1):
+            t = keep.tile([P, (b1 - b0) * TILES, GROUP], BF16, name="a_%d_%d" % (g, b0), align_bytes=64)
+            src = a[b0 * GROUP : b1 * GROUP, g * GROUP : (g + 1) * GROUP]
+            nc.sync.dma_start(out=t[:], in_=src.rearrange("(j p) n -> p j n", p=P))
+            for b in range(b0, b1):
+                a_sb[(g, b)] = (t, (b - b0) * TILES)
+
+        def load_c(b0, b1):
+            t = keep.tile([P, PASSES, (b1 - b0) * GROUP], U32, name="c_%d" % b0, align_bytes=64)
+            src = c_words.rearrange("c p m t -> p c (m t)")[:, :, b0 * GROUP * PACK : b1 * GROUP * PACK]
+            nc.sync.dma_start(out=t[:].bitcast(I32), in_=src.bitcast(I32))
+            for b in range(b0, b1):
+                c_sb[b] = (t, (b - b0) * GROUP)
+
+        load_r(0)
+        load_c(0, 1)
+        for q in range(4):
+            nc.sync.dma_start(
+                out=c_plane[32 * q : 32 * q + 4, :, :].bitcast(I32),
+                in_=c_scales[:, 4 * q : 4 * q + 4, :].rearrange("c r m -> r c m").bitcast(I32),
+            )
+        load_a(0, 0, 1)
+        load_a(0, 1, 2)
+        load_c(1, 2)
+        load_r(1)
+        load_a(0, 2, 3)
+        load_c(2, 3)
+        load_a(1, 0, BANDS)
+        load_r(2)
+        load_a(2, 0, BANDS)
+        load_r(3)
+        load_a(3, 0, BANDS)
+
+        w_f32 = keep.tile([P, P], F32, name="w_f32")
+        w_pos = keep.tile([P, M // P], F32, name="w_pos")
+        w_neg = keep.tile([P, M // P], F32, name="w_neg")
+
+        def spread_w():
+            w_ps = turns.tile([P, 2, HALF], F32, name="turn")
+            nc.tensor.transpose(w_ps[:, 0, :P], w_f32[:], ident[:])
+            nc.scalar.activation(out=w_pos[:], in_=w_ps[:, 0, : M // P], func=COPY)
+            nc.scalar.activation(out=w_neg[:], in_=w_ps[:, 0, : M // P], func=COPY, scale=-1.0)
+
+        ur_codes = keep.tile([P, GROUPS * PASSES, GROUP], U32, name="ur_codes", align_bytes=64)
+        ur_plane = keep.tile([P, GROUPS * PASSES, GROUP], U8, name="ur_plane", align_bytes=64)
+        y_plane = keep.tile([P, M], U8, name="y_plane", align_bytes=64)
+        side = {}
+        y_sb = {}
+        acc = {}
+        y_bf = {}
+        turned = {}
+        y_t = {}
+
+        def scale_r(g, c):
+            t = r_sb[(g, c)]
+            for s in range(PACK):
+                nc.vector.tensor_scalar(out=t[:, s, :], in0=t[:, s, :], scalar1=core_sb[:, c, s : s + 1], scalar2=None, op0=MULT)
+
+        def weave_r(g, n0, n1, on_scalar):
+            for c in range(PASSES):
+                lo, hi = max(n0 - c * GROUP, 0), min(n1 - c * GROUP, GROUP)
+                if lo >= hi:
+                    continue
+                if (g, c) not in side:
+                    side[(g, c)] = ring.tile([P, GROUP, PACK], BF16, name="side", align_bytes=64)
+                dst = side[(g, c)][:, lo:hi, :].rearrange("p (n i) t -> p n t i", i=4)
+                src = r_sb[(g, c)][:, :, lo:hi].rearrange("p t (n i) -> p n t i", i=4)
+                if on_scalar:
+                    nc.scalar.copy(out=dst, in_=src)
+                else:
+                    nc.vector.tensor_copy(out=dst, in_=src)
+
+        def quant_r(g, c):
+            nc.vector.quantize_mx(
+                out=ur_codes[:, g * PASSES + c, :].bitcast(E4M3X4),
+                scales=ur_plane[:, g * PASSES + c, :],
+                in_=side[(g, c)][:].rearrange("p n t -> p (n t)"),
+            )
+
+        def weigh_a(i):
+            g, b = divmod(i, BANDS)
+            t, j0 = a_sb[(g, b)]
+            y_sb[i] = ypool.tile([P, TILES, GROUP], F32, name="y", align_bytes=64)
+            for j in range(TILES):
+                row = b * TILES + j
+                nc.scalar.activation(out=y_sb[i][:, j, :], in_=t[:, j0 + j, :], func=COPY, scale=w_pos[:, row : row + 1])
+
+        def multiply(i, order):
+            g, b = divmod(i, BANDS)
+            t, m0 = c_sb[b]
+            for j, c in order:
+                if c == 0:
+                    acc[(i, j)] = accs.tile([P, GROUP], F32, name="acc")
+                nc.tensor.matmul_mx(
+                    out=acc[(i, j)][:],
+                    lhsT=t[:, c, m0 + j * P : m0 + (j + 1) * P].bitcast(E5M2X4),
+                    lhsT_scale=c_plane[:, c, (b * TILES + j) * P : (b * TILES + j + 1) * P],
+                    rhs=ur_codes[:, g * PASSES + c, :].bitcast(E4M3X4),
+                    rhs_scale=ur_plane[:, g * PASSES + c, :],
+                    start=(c == 0),
+                    stop=(c == PASSES - 1),
+                )
+
+        by_tile = [(j, c) for j in range(TILES) for c in range(PASSES)]
+        by_pass = [(j, c) for c in range(PASSES) for j in range(TILES)]
+
+        def subtract(i, j0, j1):
+            g, b = divmod(i, BANDS)
+            for j in range(j0, j1):
+                row = b * TILES + j
+                nc.vector.scalar_tensor_tensor(
+                    out=y_sb[i][:, j, :], in0=acc[(i, j)][:], scalar=w_neg[:, row : row + 1], in1=y_sb[i][:, j, :], op0=MULT, op1=ADD
+                )
+            dst = out_0[b * GROUP + j0 * P : b * GROUP + j1 * P, g * GROUP : (g + 1) * GROUP]
+            nc.sync.dma_start(out=dst.rearrange("(j p) n -> p j n", p=P), in_=y_sb[i][:, j0:j1, :])
+
+        def round_y(i, j0, j1, on_scalar):
+            if i not in y_bf:
+                y_bf[i] = ring.tile([P, TILES, GROUP], BF16, name="y_bf", align_bytes=64)
+            walk = "m j u p e" if (j1 - j0) % 2 == 0 else "m u j p e"
+            dst = y_bf[i][:, j0:j1, :].rearrange("m j (u p e) -> " + walk, u=2, e=2)
+            src = y_sb[i][:, j0:j1, :].rearrange("m j (p u e) -> " + walk, u=2, e=2)
+            if on_scalar:
+                nc.scalar.copy(out=dst, in_=src)
+            else:
+                nc.vector.tensor_copy(out=dst, in_=src)
+
+        def turn_y(i, j0, j1):
+            words = y_bf[i][:].bitcast(F32)
+            turned[(i, j0)] = turns.tile([P, 2, HALF], F32, name="turn")
+            for j in range(j0, j1):
+                for u in range(2):
+                    nc.tensor.transpose(
+                        turned[(i, j0)][:, u, (j - j0) * P : (j - j0 + 1) * P], words[:, j, u * P : (u + 1) * P], ident[:]
+                    )
+
+        def weave_y(i, j0, j1):
+            if i not in y_t:
+                y_t[i] = ring.tile([P, GROUP, PACK], BF16, name="y_t", align_bytes=64)
+            words = y_t[i][:].bitcast(F32)
+            src = turned[(i, j0)][:, :, : (j1 - j0) * P]
+            nc.scalar.copy(out=words[:, j0 * P : j1 * P, :], in_=src.rearrange("p u m -> p m u"))
+
+        def quant_y(i, j0, j1):
+            g, b = divmod(i, BANDS)
+            m0, m1 = b * GROUP + j0 * P, b * GROUP + j1 * P
+            codes = opool.tile([P, GROUP], U32, name="y_codes", align_bytes=64)
+            nc.vector.quantize_mx(
+                out=codes[:, : m1 - m0].bitcast(E4M3X4),
+                scales=y_plane[4 * g :, m0:m1],
+                in_=y_t[i][:, j0 * P : j1 * P, :].rearrange("p m t -> p (m t)"),
+            )
+            dst = out_1[g].rearrange("p m t -> p (m t)")[:, m0 * PACK : m1 * PACK]
+            nc.sync.dma_start(out=dst.bitcast(I32), in_=codes[:, : m1 - m0].bitcast(I32))
+
+        def store_scales(m0, m1):
+            for q in range(4):
+                nc.sync.dma_start(
+                    out=out_2[:, 4 * q : 4 * q + 4, m0:m1].bitcast(I32),
+                    in_=y_plane[32 * q : 32 * q + 16, m0:m1].bitcast(I32),
+                )
+
+        scale_r(0, 0)
+        weave_r(0, 0, HALF, False)
+        weave_r(0, HALF, GROUP, True)
+        scale_r(0, 1)
+        nc.vector.tensor_copy(out=w_f32[:], in_=w_rows[:])
+        quant_r(0, 0)
+        weave_r(0, GROUP, GROUP + HALF, False)
+        weave_r(0, GROUP + HALF, 2 * GROUP, True)
+        spread_w()
+        quant_r(0, 1)
+        weigh_a(0)
+        multiply(0, [(0, 0), (1, 0), (0, 1), (1, 1)] + by_tile[4:])
+
+        last = UNITS - 1
+        for i in range(last):
+            shared = i >= SHARED_FROM
+            subtract(i, 0, TILES)
+            if i % BANDS == BANDS - 1:
+                quant_r(i // BANDS + 1, 1)
+            multiply(i + 1, by_tile)
+            if not shared:
+                weigh_a(i + 1)
+            if i > 0:
+                weave_y(i - 1, 0, 2)
+                weave_y(i - 1, 2, 4)
+            for g in range(1, GROUPS):
+                for c in range(PASSES):
+                    if i == max(0, BANDS * g - 4 + c):
+                        scale_r(g, c)
+            if shared:
+                round_y(i, 0, 1, True)
+                quant_y(i - 1, 0, TILES)
+                round_y(i, 1, TILES, False)
+                weigh_a(i + 1)
+            else:
+                round_y(i, 0, TILES, False)
+            turn_y(i, 0, 2)
+            turn_y(i, 2, 4)
+            if i > 0 and not shared:
+                quant_y(i - 1, 0, TILES)
+            for g in range(1, GROUPS):
+                for k in range(BANDS):
+                    if i == max(0, BANDS * g - 4 + k):
+                        weave_r(g, k * RUN, (k + 1) * RUN, True)
+                if i == BANDS * g - 2:
+                    quant_r(g, 0)
+                    weave_r(g, BANDS * RUN, PASSES * GROUP, False)
+
+        weave_y(last - 1, 0, 2)
+        weave_y(last - 1, 2, 4)
+        subtract(last, 0, 1)
+        subtract(last, 1, 2)
+        round_y(last, 0, 2, True)
+        turn_y(last, 0, 2)
+        subtract(last, 2, 3)
+        subtract(last, 3, 4)
+        round_y(last, 2, 3, False)
+        round_y(last, 3, 4, False)
+        turn_y(last, 2, 4)
+        quant_y(last - 1, 0, TILES)
+        weave_y(last, 0, 2)
+        quant_y(last, 0, 2)
+        weave_y(last, 2, 4)
+        quant_y(last, 2, 4)
+        store_scales(0, M)

@@ -15,6 +15,7 @@ E4M3X4 = mybir.dt.float8_e4m3fn_x4
 E5M2X4 = mybir.dt.float8_e5m2_x4
 MULT = mybir.AluOpType.mult
 ADD = mybir.AluOpType.add
+SUB = mybir.AluOpType.subtract
 COPY = mybir.ActivationFunctionType.Copy
 
 P = 128
@@ -22,12 +23,12 @@ PACK = 4
 GROUP = P * PACK
 PASSES = K // GROUP
 GROUPS = N // GROUP
-TILES = 4
-BANDS = M // (TILES * P)
-UNITS = GROUPS * BANDS
-HALF = GROUP // 2
-RUN = 288
-SHARED_FROM = 7
+TILES = M // P
+CODE_STORES = ((0, 4), (4, 8), (8, 10), (10, 11), (11, 12))
+AHEAD = 2
+WEAVE_SCALAR = 320
+POOL_GROUPS = 2
+ROUND_SCALAR = 2
 
 
 def tile_cur_residual_planes_k2_kernel(tc, a, c_words, c_scales, core, r, row_weight, out_0, out_1, out_2):
@@ -36,8 +37,7 @@ def tile_cur_residual_planes_k2_kernel(tc, a, c_words, c_scales, core, r, row_we
         keep = ctx.enter_context(tc.tile_pool(name="keep", bufs=1))
         ypool = ctx.enter_context(tc.tile_pool(name="ypool", bufs=8))
         ring = ctx.enter_context(tc.tile_pool(name="ring", bufs=2))
-        opool = ctx.enter_context(tc.tile_pool(name="opool", bufs=8))
-        accs = ctx.enter_context(tc.psum_pool(name="accs", bufs=TILES))
+        accs = ctx.enter_context(tc.psum_pool(name="accs", bufs=GROUPS))
         turns = ctx.enter_context(tc.psum_pool(name="turns", bufs=4))
         ctx.enter_context(tc.manual_schedule())
 
@@ -52,7 +52,7 @@ def tile_cur_residual_planes_k2_kernel(tc, a, c_words, c_scales, core, r, row_we
         nc.scalar.dma_start(out=core_bf[:], in_=core.rearrange("(c p t) -> p c t", c=PASSES, t=PACK))
         w_src = row_weight.rearrange("(j p) -> j p", p=P)
         nc.scalar.dma_start(out=w_rows[:8, :], in_=w_src[:8, :])
-        nc.scalar.dma_start(out=w_rows[8 : M // P, :], in_=w_src[8:, :])
+        nc.scalar.dma_start(out=w_rows[8:TILES, :], in_=w_src[8:, :])
         core_sb = keep.tile([P, PASSES, PACK], F32, name="core_sb")
         nc.scalar.activation(out=core_sb[:], in_=core_bf[:], func=COPY)
 
@@ -60,58 +60,62 @@ def tile_cur_residual_planes_k2_kernel(tc, a, c_words, c_scales, core, r, row_we
         a_sb = {}
         c_sb = {}
 
-        def load_r(g):
-            for c in range(PASSES):
-                t = keep.tile([P, PACK, GROUP], BF16, name="r_%d_%d" % (g, c), align_bytes=64)
-                src = r[c * GROUP : (c + 1) * GROUP, g * GROUP : (g + 1) * GROUP]
-                nc.sync.dma_start(out=t[:], in_=src.rearrange("(p t) n -> p t n", t=PACK))
-                r_sb[(g, c)] = t
+        def load_r(c, g0, g1):
+            t = keep.tile([P, PACK, (g1 - g0) * GROUP], BF16, name="r_%d_%d" % (c, g0), align_bytes=64)
+            src = r[c * GROUP : (c + 1) * GROUP, g0 * GROUP : g1 * GROUP]
+            nc.sync.dma_start(out=t[:], in_=src.rearrange("(p t) n -> p t n", t=PACK))
+            for g in range(g0, g1):
+                r_sb[(c, g)] = (t, (g - g0) * GROUP)
 
-        def load_a(g, b0, b1):
-            t = keep.tile([P, (b1 - b0) * TILES, GROUP], BF16, name="a_%d_%d" % (g, b0), align_bytes=64)
-            src = a[b0 * GROUP : b1 * GROUP, g * GROUP : (g + 1) * GROUP]
-            nc.sync.dma_start(out=t[:], in_=src.rearrange("(j p) n -> p j n", p=P))
-            for b in range(b0, b1):
-                a_sb[(g, b)] = (t, (b - b0) * TILES)
+        def load_a(j0, j1):
+            t = keep.tile([P, j1 - j0, N], BF16, name="a_%d" % j0, align_bytes=64)
+            nc.sync.dma_start(out=t[:], in_=a[j0 * P : j1 * P, :].rearrange("(j p) n -> p j n", p=P))
+            for j in range(j0, j1):
+                a_sb[j] = t[:, j - j0, :]
 
-        def load_c(b0, b1):
-            t = keep.tile([P, PASSES, (b1 - b0) * GROUP], U32, name="c_%d" % b0, align_bytes=64)
-            src = c_words.rearrange("c p m t -> p c (m t)")[:, :, b0 * GROUP * PACK : b1 * GROUP * PACK]
+        def load_c(j0, j1):
+            t = keep.tile([P, PASSES, (j1 - j0) * P], U32, name="c_%d" % j0, align_bytes=64)
+            src = c_words.rearrange("c p m t -> p c (m t)")[:, :, j0 * P * PACK : j1 * P * PACK]
             nc.sync.dma_start(out=t[:].bitcast(I32), in_=src.bitcast(I32))
-            for b in range(b0, b1):
-                c_sb[b] = (t, (b - b0) * GROUP)
+            for j in range(j0, j1):
+                c_sb[j] = t[:, :, (j - j0) * P : (j - j0 + 1) * P]
 
-        load_r(0)
-        load_c(0, 1)
+        load_r(0, 0, 1)
+        load_r(0, 1, 2)
+        load_r(0, 2, 3)
+        load_r(0, 3, 4)
+        load_r(1, 0, 2)
+        load_r(1, 2, 4)
         for q in range(4):
             nc.sync.dma_start(
                 out=c_plane[32 * q : 32 * q + 4, :, :].bitcast(I32),
                 in_=c_scales[:, 4 * q : 4 * q + 4, :].rearrange("c r m -> r c m").bitcast(I32),
             )
-        load_a(0, 0, 1)
-        load_a(0, 1, 2)
-        load_c(1, 2)
-        load_r(1)
-        load_a(0, 2, 3)
-        load_c(2, 3)
-        load_a(1, 0, BANDS)
-        load_r(2)
-        load_a(2, 0, BANDS)
-        load_r(3)
-        load_a(3, 0, BANDS)
+        load_a(0, 1)
+        load_c(0, 4)
+        load_a(1, 2)
+        load_a(2, 4)
+        load_c(4, TILES)
+        load_a(4, 8)
+        load_a(8, TILES)
 
         w_f32 = keep.tile([P, P], F32, name="w_f32")
-        w_pos = keep.tile([P, M // P], F32, name="w_pos")
-        w_neg = keep.tile([P, M // P], F32, name="w_neg")
+        w_pos = keep.tile([P, TILES], F32, name="w_pos")
+        w_neg = keep.tile([P, TILES], F32, name="w_neg")
 
         def spread_w():
-            w_ps = turns.tile([P, 2, HALF], F32, name="turn")
-            nc.tensor.transpose(w_ps[:, 0, :P], w_f32[:], ident[:])
-            nc.scalar.activation(out=w_pos[:], in_=w_ps[:, 0, : M // P], func=COPY)
-            nc.scalar.activation(out=w_neg[:], in_=w_ps[:, 0, : M // P], func=COPY, scale=-1.0)
+            w_ps = turns.tile([P, 2, 2, P], F32, name="turn")
+            nc.tensor.transpose(w_ps[:, 0, 0, :], w_f32[:], ident[:])
+            nc.scalar.activation(out=w_pos[:], in_=w_ps[:, 0, 0, :TILES], func=COPY)
+            nc.scalar.activation(out=w_neg[:], in_=w_ps[:, 0, 0, :TILES], func=COPY, scale=-1.0)
 
-        ur_codes = keep.tile([P, GROUPS * PASSES, GROUP], U32, name="ur_codes", align_bytes=64)
-        ur_plane = keep.tile([P, GROUPS * PASSES, GROUP], U8, name="ur_plane", align_bytes=64)
+        ur_codes = keep.tile([P, PASSES * GROUPS, GROUP], U32, name="ur_codes", align_bytes=64)
+        ur_plane = keep.tile([P, PASSES * GROUPS, GROUP], U8, name="ur_plane", align_bytes=64)
+        y_codes = {}
+        for j0, j1 in CODE_STORES:
+            t = keep.tile([P, GROUPS, (j1 - j0) * P], U32, name="y_codes_%d" % j0, align_bytes=64)
+            for j in range(j0, j1):
+                y_codes[j] = (t, j0, j1)
         y_plane = keep.tile([P, M], U8, name="y_plane", align_bytes=64)
         side = {}
         y_sb = {}
@@ -120,177 +124,171 @@ def tile_cur_residual_planes_k2_kernel(tc, a, c_words, c_scales, core, r, row_we
         turned = {}
         y_t = {}
 
-        def scale_r(g, c):
-            t = r_sb[(g, c)]
+        def scale_r(c, g):
+            t, n0 = r_sb[(c, g)]
             for s in range(PACK):
-                nc.vector.tensor_scalar(out=t[:, s, :], in0=t[:, s, :], scalar1=core_sb[:, c, s : s + 1], scalar2=None, op0=MULT)
+                rows = t[:, s, n0 : n0 + GROUP]
+                nc.vector.tensor_scalar(out=rows, in0=rows, scalar1=core_sb[:, c, s : s + 1], scalar2=None, op0=MULT)
 
-        def weave_r(g, n0, n1, on_scalar):
-            for c in range(PASSES):
-                lo, hi = max(n0 - c * GROUP, 0), min(n1 - c * GROUP, GROUP)
-                if lo >= hi:
-                    continue
-                if (g, c) not in side:
-                    side[(g, c)] = ring.tile([P, GROUP, PACK], BF16, name="side", align_bytes=64)
-                dst = side[(g, c)][:, lo:hi, :].rearrange("p (n i) t -> p n t i", i=4)
-                src = r_sb[(g, c)][:, :, lo:hi].rearrange("p t (n i) -> p n t i", i=4)
-                if on_scalar:
+        def weave_r(c, g):
+            t, n0 = r_sb[(c, g)]
+            side[(c, g)] = ring.tile([P, GROUP, PACK], BF16, name="side", bufs=3, align_bytes=64)
+            for lo, hi in ((0, WEAVE_SCALAR), (WEAVE_SCALAR, GROUP)):
+                dst = side[(c, g)][:, lo:hi, :].rearrange("p (n i) t -> p n t i", i=4)
+                src = t[:, :, n0 + lo : n0 + hi].rearrange("p t (n i) -> p n t i", i=4)
+                if lo == 0:
                     nc.scalar.copy(out=dst, in_=src)
                 else:
                     nc.vector.tensor_copy(out=dst, in_=src)
 
-        def quant_r(g, c):
+        def quant_r(c, g):
             nc.vector.quantize_mx(
-                out=ur_codes[:, g * PASSES + c, :].bitcast(E4M3X4),
-                scales=ur_plane[:, g * PASSES + c, :],
-                in_=side[(g, c)][:].rearrange("p n t -> p (n t)"),
+                out=ur_codes[:, c * GROUPS + g, :].bitcast(E4M3X4),
+                scales=ur_plane[:, c * GROUPS + g, :],
+                in_=side[(c, g)][:].rearrange("p n t -> p (n t)"),
             )
 
-        def weigh_a(i):
-            g, b = divmod(i, BANDS)
-            t, j0 = a_sb[(g, b)]
-            y_sb[i] = ypool.tile([P, TILES, GROUP], F32, name="y", align_bytes=64)
-            for j in range(TILES):
-                row = b * TILES + j
-                nc.scalar.activation(out=y_sb[i][:, j, :], in_=t[:, j0 + j, :], func=COPY, scale=w_pos[:, row : row + 1])
+        def weigh_a(j, g0, g1):
+            if j not in y_sb:
+                y_sb[j] = ypool.tile([P, N], F32, name="y", align_bytes=64)
+            n0, n1 = max(g0, POOL_GROUPS) * GROUP, g1 * GROUP
+            if n0 < n1:
+                nc.scalar.activation(out=y_sb[j][:, n0:n1], in_=a_sb[j][:, n0:n1], func=COPY, scale=w_pos[:, j : j + 1])
 
-        def multiply(i, order):
-            g, b = divmod(i, BANDS)
-            t, m0 = c_sb[b]
-            for j, c in order:
+        def multiply(j, order):
+            for g, c in order:
                 if c == 0:
-                    acc[(i, j)] = accs.tile([P, GROUP], F32, name="acc")
+                    acc[(j, g)] = accs.tile([P, GROUP], F32, name="acc")
                 nc.tensor.matmul_mx(
-                    out=acc[(i, j)][:],
-                    lhsT=t[:, c, m0 + j * P : m0 + (j + 1) * P].bitcast(E5M2X4),
-                    lhsT_scale=c_plane[:, c, (b * TILES + j) * P : (b * TILES + j + 1) * P],
-                    rhs=ur_codes[:, g * PASSES + c, :].bitcast(E4M3X4),
-                    rhs_scale=ur_plane[:, g * PASSES + c, :],
+                    out=acc[(j, g)][:],
+                    lhsT=c_sb[j][:, c, :].bitcast(E5M2X4),
+                    lhsT_scale=c_plane[:, c, j * P : (j + 1) * P],
+                    rhs=ur_codes[:, c * GROUPS + g, :].bitcast(E4M3X4),
+                    rhs_scale=ur_plane[:, c * GROUPS + g, :],
                     start=(c == 0),
                     stop=(c == PASSES - 1),
                 )
 
-        by_tile = [(j, c) for j in range(TILES) for c in range(PASSES)]
-        by_pass = [(j, c) for c in range(PASSES) for j in range(TILES)]
+        by_group = [(g, c) for g in range(GROUPS) for c in range(PASSES)]
 
-        def subtract(i, j0, j1):
-            g, b = divmod(i, BANDS)
-            for j in range(j0, j1):
-                row = b * TILES + j
-                nc.vector.scalar_tensor_tensor(
-                    out=y_sb[i][:, j, :], in0=acc[(i, j)][:], scalar=w_neg[:, row : row + 1], in1=y_sb[i][:, j, :], op0=MULT, op1=ADD
-                )
-            dst = out_0[b * GROUP + j0 * P : b * GROUP + j1 * P, g * GROUP : (g + 1) * GROUP]
-            nc.sync.dma_start(out=dst.rearrange("(j p) n -> p j n", p=P), in_=y_sb[i][:, j0:j1, :])
+        def subtract(j, g0, g1):
+            for g in range(g0, g1):
+                cols = slice(g * GROUP, (g + 1) * GROUP)
+                y = y_sb[j][:, cols]
+                if g < POOL_GROUPS:
+                    nc.vector.tensor_tensor(out=y, in0=a_sb[j][:, cols], in1=acc[(j, g)][:], op=SUB)
+                    nc.gpsimd.tensor_scalar(out=y, in0=y, scalar1=w_pos[:, j : j + 1], scalar2=0.0, op0=MULT, op1=ADD)
+                else:
+                    nc.vector.scalar_tensor_tensor(out=y, in0=acc[(j, g)][:], scalar=w_neg[:, j : j + 1], in1=y, op0=MULT, op1=ADD)
 
-        def round_y(i, j0, j1, on_scalar):
-            if i not in y_bf:
-                y_bf[i] = ring.tile([P, TILES, GROUP], BF16, name="y_bf", align_bytes=64)
-            walk = "m j u p e" if (j1 - j0) % 2 == 0 else "m u j p e"
-            dst = y_bf[i][:, j0:j1, :].rearrange("m j (u p e) -> " + walk, u=2, e=2)
-            src = y_sb[i][:, j0:j1, :].rearrange("m j (p u e) -> " + walk, u=2, e=2)
+        def store_y(j, g0, g1):
+            cols = slice(g0 * GROUP, g1 * GROUP)
+            nc.sync.dma_start(out=out_0[j * P : (j + 1) * P, cols], in_=y_sb[j][:, cols])
+
+        def round_y(j, g0, g1, on_scalar):
+            if j not in y_bf:
+                y_bf[j] = ring.tile([P, GROUPS, GROUP], BF16, name="y_bf", align_bytes=64)
+            walk = "m g u p e" if (g1 - g0) % 2 == 0 else "m u g p e"
+            dst = y_bf[j][:, g0:g1, :].rearrange("m g (u p e) -> " + walk, u=2, e=2)
+            src = y_sb[j][:, g0 * GROUP : g1 * GROUP].rearrange("m (g p u e) -> " + walk, p=P, u=2, e=2)
             if on_scalar:
                 nc.scalar.copy(out=dst, in_=src)
             else:
                 nc.vector.tensor_copy(out=dst, in_=src)
 
-        def turn_y(i, j0, j1):
-            words = y_bf[i][:].bitcast(F32)
-            turned[(i, j0)] = turns.tile([P, 2, HALF], F32, name="turn")
-            for j in range(j0, j1):
+        def turn_y(j, h):
+            words = y_bf[j][:].bitcast(F32)
+            turned[(j, h)] = turns.tile([P, 2, 2, P], F32, name="turn")
+            for g in range(2):
                 for u in range(2):
-                    nc.tensor.transpose(
-                        turned[(i, j0)][:, u, (j - j0) * P : (j - j0 + 1) * P], words[:, j, u * P : (u + 1) * P], ident[:]
-                    )
+                    nc.tensor.transpose(turned[(j, h)][:, g, u, :], words[:, 2 * h + g, u * P : (u + 1) * P], ident[:])
 
-        def weave_y(i, j0, j1):
-            if i not in y_t:
-                y_t[i] = ring.tile([P, GROUP, PACK], BF16, name="y_t", align_bytes=64)
-            words = y_t[i][:].bitcast(F32)
-            src = turned[(i, j0)][:, :, : (j1 - j0) * P]
-            nc.scalar.copy(out=words[:, j0 * P : j1 * P, :], in_=src.rearrange("p u m -> p m u"))
+        def weave_y(j, h):
+            if j not in y_t:
+                y_t[j] = ring.tile([P, GROUPS, P, PACK], BF16, name="y_t", align_bytes=64)
+            words = y_t[j][:].bitcast(F32)
+            nc.scalar.copy(out=words[:, 2 * h : 2 * h + 2, :, :], in_=turned[(j, h)][:].rearrange("p g u m -> p g m u"))
 
-        def quant_y(i, j0, j1):
-            g, b = divmod(i, BANDS)
-            m0, m1 = b * GROUP + j0 * P, b * GROUP + j1 * P
-            codes = opool.tile([P, GROUP], U32, name="y_codes", align_bytes=64)
-            nc.vector.quantize_mx(
-                out=codes[:, : m1 - m0].bitcast(E4M3X4),
-                scales=y_plane[4 * g :, m0:m1],
-                in_=y_t[i][:, j0 * P : j1 * P, :].rearrange("p m t -> p (m t)"),
-            )
-            dst = out_1[g].rearrange("p m t -> p (m t)")[:, m0 * PACK : m1 * PACK]
-            nc.sync.dma_start(out=dst.bitcast(I32), in_=codes[:, : m1 - m0].bitcast(I32))
+        def quant_y(j, g0, g1):
+            t, j0, j1 = y_codes[j]
+            for g in range(g0, g1):
+                nc.vector.quantize_mx(
+                    out=t[:, g, (j - j0) * P : (j - j0 + 1) * P].bitcast(E4M3X4),
+                    scales=y_plane[4 * g :, j * P : (j + 1) * P],
+                    in_=y_t[j][:, g, :, :].rearrange("p m t -> p (m t)"),
+                )
+            if g1 == GROUPS and j == j1 - 1:
+                dst = out_1.rearrange("g p m t -> p g (m t)")[:, :, j0 * P * PACK : j1 * P * PACK]
+                nc.sync.dma_start(out=dst.bitcast(I32), in_=t[:].bitcast(I32))
 
-        def store_scales(m0, m1):
+        def store_scales():
             for q in range(4):
                 nc.sync.dma_start(
-                    out=out_2[:, 4 * q : 4 * q + 4, m0:m1].bitcast(I32),
-                    in_=y_plane[32 * q : 32 * q + 16, m0:m1].bitcast(I32),
+                    out=out_2[:, 4 * q : 4 * q + 4, :].bitcast(I32),
+                    in_=y_plane[32 * q : 32 * q + 16, :].bitcast(I32),
                 )
 
+        steps = [(c, g) for c in range(PASSES) for g in range(GROUPS)]
         scale_r(0, 0)
-        weave_r(0, 0, HALF, False)
-        weave_r(0, HALF, GROUP, True)
-        scale_r(0, 1)
-        nc.vector.tensor_copy(out=w_f32[:], in_=w_rows[:])
-        quant_r(0, 0)
-        weave_r(0, GROUP, GROUP + HALF, False)
-        weave_r(0, GROUP + HALF, 2 * GROUP, True)
-        spread_w()
-        quant_r(0, 1)
-        weigh_a(0)
-        multiply(0, [(0, 0), (1, 0), (0, 1), (1, 1)] + by_tile[4:])
+        for s in range(len(steps)):
+            weave_r(*steps[s])
+            if s == PASSES * GROUPS - 3:
+                nc.vector.tensor_copy(out=w_f32[:], in_=w_rows[:])
+                spread_w()
+            if s + 1 < len(steps):
+                scale_r(*steps[s + 1])
+            if s > 0:
+                quant_r(*steps[s - 1])
+            if s == PASSES * GROUPS - 2:
+                weigh_a(0, 0, 2)
+        quant_r(*steps[-1])
+        weigh_a(0, 2, 4)
+        multiply(0, by_group)
 
-        last = UNITS - 1
-        for i in range(last):
-            shared = i >= SHARED_FROM
-            subtract(i, 0, TILES)
-            if i % BANDS == BANDS - 1:
-                quant_r(i // BANDS + 1, 1)
-            multiply(i + 1, by_tile)
-            if not shared:
-                weigh_a(i + 1)
-            if i > 0:
-                weave_y(i - 1, 0, 2)
-                weave_y(i - 1, 2, 4)
-            for g in range(1, GROUPS):
-                for c in range(PASSES):
-                    if i == max(0, BANDS * g - 4 + c):
-                        scale_r(g, c)
-            if shared:
-                round_y(i, 0, 1, True)
-                quant_y(i - 1, 0, TILES)
-                round_y(i, 1, TILES, False)
-                weigh_a(i + 1)
-            else:
-                round_y(i, 0, TILES, False)
-            turn_y(i, 0, 2)
-            turn_y(i, 2, 4)
-            if i > 0 and not shared:
-                quant_y(i - 1, 0, TILES)
-            for g in range(1, GROUPS):
-                for k in range(BANDS):
-                    if i == max(0, BANDS * g - 4 + k):
-                        weave_r(g, k * RUN, (k + 1) * RUN, True)
-                if i == BANDS * g - 2:
-                    quant_r(g, 0)
-                    weave_r(g, BANDS * RUN, PASSES * GROUP, False)
+        last = TILES - 1
+        for j in range(last):
+            subtract(j, 0, 1)
+            if j > 1:
+                quant_y(j - 2, 3, 4)
+            subtract(j, 1, GROUPS)
+            store_y(j, 0, GROUPS)
+            multiply(j + 1, by_group)
+            if j == 0:
+                weigh_a(1, 0, 4)
+            if j + AHEAD < TILES:
+                weigh_a(j + AHEAD, 0, 4)
+            if j > 0:
+                weave_y(j - 1, 0)
+                weave_y(j - 1, 1)
+            for g in range(ROUND_SCALAR):
+                round_y(j, g, g + 1, True)
+            for g in range(GROUPS - 1):
+                if j > 0:
+                    quant_y(j - 1, g, g + 1)
+                if ROUND_SCALAR + g < GROUPS:
+                    round_y(j, ROUND_SCALAR + g, ROUND_SCALAR + g + 1, False)
+            turn_y(j, 0)
+            turn_y(j, 1)
 
-        weave_y(last - 1, 0, 2)
-        weave_y(last - 1, 2, 4)
+        weave_y(last - 1, 0)
+        weave_y(last - 1, 1)
         subtract(last, 0, 1)
+        quant_y(last - 2, 3, 4)
         subtract(last, 1, 2)
-        round_y(last, 0, 2, True)
-        turn_y(last, 0, 2)
-        subtract(last, 2, 3)
-        subtract(last, 3, 4)
-        round_y(last, 2, 3, False)
-        round_y(last, 3, 4, False)
-        turn_y(last, 2, 4)
-        quant_y(last - 1, 0, TILES)
-        weave_y(last, 0, 2)
-        quant_y(last, 0, 2)
-        weave_y(last, 2, 4)
-        quant_y(last, 2, 4)
-        store_scales(0, M)
+        store_y(last, 0, 2)
+        round_y(last, 0, 1, True)
+        round_y(last, 1, 2, True)
+        turn_y(last, 0)
+        subtract(last, 2, 4)
+        store_y(last, 2, 4)
+        for g in range(2):
+            quant_y(last - 1, g, g + 1)
+            round_y(last, 2 + g, 3 + g, False)
+        turn_y(last, 1)
+        weave_y(last, 0)
+        weave_y(last, 1)
+        quant_y(last - 1, 2, 3)
+        quant_y(last, 0, 1)
+        quant_y(last - 1, 3, 4)
+        quant_y(last, 1, 4)
+        store_scales()

@@ -24,18 +24,17 @@ GROUP = P * PACK
 PASSES = K // GROUP
 GROUPS = N // GROUP
 TILES = M // P
-CODE_STORES = ((0, 4), (4, 8), (8, 10), (10, 11), (11, 12))
+CODE_STORES = ((0, 5), (5, 7), (7, 9), (9, 11), (11, 12))
 AHEAD = 2
 WEAVE_SCALAR = 320
 POOL_GROUPS = 2
-ROUND_SCALAR = 2
 
 
 def tile_cur_residual_planes_k2_kernel(tc, a, c_words, c_scales, core, r, row_weight, out_0, out_1, out_2):
     nc = tc.nc
     with ExitStack() as ctx:
         keep = ctx.enter_context(tc.tile_pool(name="keep", bufs=1))
-        ypool = ctx.enter_context(tc.tile_pool(name="ypool", bufs=8))
+        ypool = ctx.enter_context(tc.tile_pool(name="ypool", bufs=7))
         ring = ctx.enter_context(tc.tile_pool(name="ring", bufs=2))
         accs = ctx.enter_context(tc.psum_pool(name="accs", bufs=GROUPS))
         turns = ctx.enter_context(tc.psum_pool(name="turns", bufs=4))
@@ -117,6 +116,8 @@ def tile_cur_residual_planes_k2_kernel(tc, a, c_words, c_scales, core, r, row_we
             for j in range(j0, j1):
                 y_codes[j] = (t, j0, j1)
         y_plane = keep.tile([P, M], U8, name="y_plane", align_bytes=64)
+        batches = [(0, 1)] + [(j, j + 2) for j in range(1, TILES - 1, 2)] + [(TILES - 1, TILES)]
+        batch_of = {j: b for b in batches for j in range(*b)}
         side = {}
         y_sb = {}
         acc = {}
@@ -151,9 +152,8 @@ def tile_cur_residual_planes_k2_kernel(tc, a, c_words, c_scales, core, r, row_we
         def weigh_a(j, g0, g1):
             if j not in y_sb:
                 y_sb[j] = ypool.tile([P, N], F32, name="y", align_bytes=64)
-            n0, n1 = max(g0, POOL_GROUPS) * GROUP, g1 * GROUP
-            if n0 < n1:
-                nc.scalar.activation(out=y_sb[j][:, n0:n1], in_=a_sb[j][:, n0:n1], func=COPY, scale=w_pos[:, j : j + 1])
+            cols = slice(g0 * GROUP, g1 * GROUP)
+            nc.scalar.activation(out=y_sb[j][:, cols], in_=a_sb[j][:, cols], func=COPY, scale=w_pos[:, j : j + 1])
 
         def multiply(j, order):
             for g, c in order:
@@ -175,7 +175,7 @@ def tile_cur_residual_planes_k2_kernel(tc, a, c_words, c_scales, core, r, row_we
             for g in range(g0, g1):
                 cols = slice(g * GROUP, (g + 1) * GROUP)
                 y = y_sb[j][:, cols]
-                if g < POOL_GROUPS:
+                if g < POOL_GROUPS and j < TILES - 1:
                     nc.vector.tensor_tensor(out=y, in0=a_sb[j][:, cols], in1=acc[(j, g)][:], op=SUB)
                     nc.gpsimd.tensor_scalar(out=y, in0=y, scalar1=w_pos[:, j : j + 1], scalar2=0.0, op0=MULT, op1=ADD)
                 else:
@@ -188,44 +188,48 @@ def tile_cur_residual_planes_k2_kernel(tc, a, c_words, c_scales, core, r, row_we
         def round_y(j, g0, g1, on_scalar):
             if j not in y_bf:
                 y_bf[j] = ring.tile([P, GROUPS, GROUP], BF16, name="y_bf", align_bytes=64)
-            walk = "m g u p e" if (g1 - g0) % 2 == 0 else "m u g p e"
-            dst = y_bf[j][:, g0:g1, :].rearrange("m g (u p e) -> " + walk, u=2, e=2)
-            src = y_sb[j][:, g0 * GROUP : g1 * GROUP].rearrange("m (g p u e) -> " + walk, p=P, u=2, e=2)
+            if g1 - g0 == 1:
+                dst = y_bf[j][:, g0, :].rearrange("m (u h p e) -> m h u p e", h=2, u=2, e=2)
+            else:
+                dst = y_bf[j][:, g0:g1, :].rearrange("m h (u p e) -> m h u p e", u=2, e=2)
+            src = y_sb[j][:, g0 * GROUP : g1 * GROUP].rearrange("m (h p u e) -> m h u p e", h=2, u=2, e=2)
             if on_scalar:
                 nc.scalar.copy(out=dst, in_=src)
             else:
                 nc.vector.tensor_copy(out=dst, in_=src)
 
-        def turn_y(j, h):
+        def turn_y(j, g0, g1):
             words = y_bf[j][:].bitcast(F32)
-            turned[(j, h)] = turns.tile([P, 2, 2, P], F32, name="turn")
-            for g in range(2):
-                for u in range(2):
-                    nc.tensor.transpose(turned[(j, h)][:, g, u, :], words[:, 2 * h + g, u * P : (u + 1) * P], ident[:])
-
-        def weave_y(j, h):
-            if j not in y_t:
-                y_t[j] = ring.tile([P, GROUPS, P, PACK], BF16, name="y_t", align_bytes=64)
-            words = y_t[j][:].bitcast(F32)
-            nc.scalar.copy(out=words[:, 2 * h : 2 * h + 2, :, :], in_=turned[(j, h)][:].rearrange("p g u m -> p g m u"))
-
-        def quant_y(j, g0, g1):
-            t, j0, j1 = y_codes[j]
+            turned[(j, g0)] = turns.tile([P, 2, 2, P], F32, name="turn")
             for g in range(g0, g1):
-                nc.vector.quantize_mx(
-                    out=t[:, g, (j - j0) * P : (j - j0 + 1) * P].bitcast(E4M3X4),
-                    scales=y_plane[4 * g :, j * P : (j + 1) * P],
-                    in_=y_t[j][:, g, :, :].rearrange("p m t -> p (m t)"),
-                )
-            if g1 == GROUPS and j == j1 - 1:
+                for u in range(2):
+                    nc.tensor.transpose(turned[(j, g0)][:, g - g0, u, :], words[:, g, u * P : (u + 1) * P], ident[:])
+
+        def weave_y(j, g0, g1):
+            first = batch_of[j][0]
+            if first not in y_t:
+                y_t[first] = ring.tile([P, GROUPS, 2 * P, PACK], BF16, name="y_t", align_bytes=64)
+            words = y_t[first][:, g0:g1, (j - first) * P : (j - first + 1) * P, :].bitcast(F32)
+            src = turned[(j, g0)][:, : g1 - g0, :, :]
+            nc.scalar.copy(out=words, in_=src.rearrange("p g u m -> p g m u"))
+
+        def quant_y(batch, g):
+            first, end = batch
+            t, j0, j1 = y_codes[first]
+            nc.vector.quantize_mx(
+                out=t[:, g, (first - j0) * P : (end - j0) * P].bitcast(E4M3X4),
+                scales=y_plane[4 * g :, first * P : end * P],
+                in_=y_t[first][:, g, : (end - first) * P, :].rearrange("p m t -> p (m t)"),
+            )
+            if g == GROUPS - 1 and end == j1:
                 dst = out_1.rearrange("g p m t -> p g (m t)")[:, :, j0 * P * PACK : j1 * P * PACK]
                 nc.sync.dma_start(out=dst.bitcast(I32), in_=t[:].bitcast(I32))
 
-        def store_scales():
+        def store_scales(j0, j1, engines):
             for q in range(4):
-                nc.sync.dma_start(
-                    out=out_2[:, 4 * q : 4 * q + 4, :].bitcast(I32),
-                    in_=y_plane[32 * q : 32 * q + 16, :].bitcast(I32),
+                engines[q % len(engines)].dma_start(
+                    out=out_2[:, 4 * q : 4 * q + 4, j0 * P : j1 * P].bitcast(I32),
+                    in_=y_plane[32 * q : 32 * q + 16, j0 * P : j1 * P].bitcast(I32),
                 )
 
         steps = [(c, g) for c in range(PASSES) for g in range(GROUPS)]
@@ -239,56 +243,63 @@ def tile_cur_residual_planes_k2_kernel(tc, a, c_words, c_scales, core, r, row_we
                 scale_r(*steps[s + 1])
             if s > 0:
                 quant_r(*steps[s - 1])
-            if s == PASSES * GROUPS - 2:
-                weigh_a(0, 0, 2)
         quant_r(*steps[-1])
-        weigh_a(0, 2, 4)
+        weigh_a(0, POOL_GROUPS, GROUPS)
         multiply(0, by_group)
 
         last = TILES - 1
+        ready = []
+
+        def quant_next():
+            if ready:
+                quant_y(*ready.pop(0))
+
         for j in range(last):
             subtract(j, 0, 1)
-            if j > 1:
-                quant_y(j - 2, 3, 4)
+            quant_next()
             subtract(j, 1, GROUPS)
             store_y(j, 0, GROUPS)
             multiply(j + 1, by_group)
             if j == 0:
-                weigh_a(1, 0, 4)
+                weigh_a(1, POOL_GROUPS, GROUPS)
             if j + AHEAD < TILES:
-                weigh_a(j + AHEAD, 0, 4)
+                weigh_a(j + AHEAD, POOL_GROUPS, GROUPS)
+            else:
+                weigh_a(last, 0, POOL_GROUPS)
             if j > 0:
-                weave_y(j - 1, 0)
-                weave_y(j - 1, 1)
-            for g in range(ROUND_SCALAR):
-                round_y(j, g, g + 1, True)
-            for g in range(GROUPS - 1):
-                if j > 0:
-                    quant_y(j - 1, g, g + 1)
-                if ROUND_SCALAR + g < GROUPS:
-                    round_y(j, ROUND_SCALAR + g, ROUND_SCALAR + g + 1, False)
-            turn_y(j, 0)
-            turn_y(j, 1)
+                weave_y(j - 1, 0, 2)
+                weave_y(j - 1, 2, 4)
+                if batch_of[j - 1][1] == j:
+                    ready.extend((batch_of[j - 1], g) for g in range(GROUPS))
+            round_y(j, 0, 2, True)
+            quant_next()
+            round_y(j, 2, 4, False)
+            turn_y(j, 0, 2)
+            turn_y(j, 2, 4)
 
-        weave_y(last - 1, 0)
-        weave_y(last - 1, 1)
+        pair, single = batches[-2], batches[-1]
+        weave_y(last - 1, 0, 2)
         subtract(last, 0, 1)
-        quant_y(last - 2, 3, 4)
+        quant_next()
+        store_scales(0, pair[0], [nc.sync])
+        round_y(last, 0, 1, True)
         subtract(last, 1, 2)
         store_y(last, 0, 2)
-        round_y(last, 0, 1, True)
         round_y(last, 1, 2, True)
-        turn_y(last, 0)
+        turn_y(last, 0, 2)
+        weave_y(last - 1, 2, 4)
         subtract(last, 2, 4)
         store_y(last, 2, 4)
+        for g in range(2, GROUPS):
+            quant_y(pair, g - 2)
+            round_y(last, g, g + 1, False)
+            turn_y(last, g, g + 1)
+        weave_y(last, 0, 2)
+        weave_y(last, 2, 3)
+        weave_y(last, 3, 4)
         for g in range(2):
-            quant_y(last - 1, g, g + 1)
-            round_y(last, 2 + g, 3 + g, False)
-        turn_y(last, 1)
-        weave_y(last, 0)
-        weave_y(last, 1)
-        quant_y(last - 1, 2, 3)
-        quant_y(last, 0, 1)
-        quant_y(last - 1, 3, 4)
-        quant_y(last, 1, 4)
-        store_scales()
+            quant_y(pair, 2 + g)
+            quant_y(single, g)
+        quant_y(single, 2)
+        quant_y(single, 3)
+        store_scales(pair[0], TILES, [nc.scalar, nc.sync])

@@ -302,4 +302,4 @@ def tile_cur_residual_planes_k2_kernel(tc, a, c_words, c_scales, core, r, row_we
             quant_y(single, g)
         quant_y(single, 2)
         quant_y(single, 3)
-        store_scales(pair[0], TILES, [nc.scalar, nc.sync])
+        store_scales(pair[0], TILES, [nc.sync])

from contextlib import ExitStack

import concourse.mybir as mybir
from concourse.masks import make_identity

M, N, K = 1536, 2048, 1024
FLOPS = 2 * M * N * K

F32 = mybir.dt.float32
BF16 = mybir.dt.bfloat16
I32 = mybir.dt.int32
U32 = mybir.dt.uint32
U8 = mybir.dt.uint8
E4M3X4 = mybir.dt.float8_e4m3fn_x4
E5M2X4 = mybir.dt.float8_e5m2_x4
MULT = mybir.AluOpType.mult
ADD = mybir.AluOpType.add
SUB = mybir.AluOpType.subtract
COPY = mybir.ActivationFunctionType.Copy

P = 128
PACK = 4
GROUP = P * PACK
PASSES = K // GROUP
GROUPS = N // GROUP
TILES = M // P
CODE_STORES = ((0, 5), (5, 7), (7, 9), (9, 11), (11, 12))
AHEAD = 2
WEAVE_SCALAR = 320
POOL_GROUPS = 2


def tile_cur_residual_planes_k2_kernel(tc, a, c_words, c_scales, core, r, row_weight, out_0, out_1, out_2):
    nc = tc.nc
    with ExitStack() as ctx:
        keep = ctx.enter_context(tc.tile_pool(name="keep", bufs=1))
        ypool = ctx.enter_context(tc.tile_pool(name="ypool", bufs=7))
        ring = ctx.enter_context(tc.tile_pool(name="ring", bufs=2))
        accs = ctx.enter_context(tc.psum_pool(name="accs", bufs=GROUPS))
        turns = ctx.enter_context(tc.psum_pool(name="turns", bufs=4))
        ctx.enter_context(tc.manual_schedule())

        ident = keep.tile([P, P], F32, name="ident")
        make_identity(nc, ident[:])
        c_plane = keep.tile([P, PASSES, M], U8, name="c_plane", align_bytes=64)
        w_rows = keep.tile([P, P], BF16, name="w_rows")
        nc.vector.memset(w_rows[:], 0.0)
        nc.vector.memset(c_plane[:].rearrange("p c m -> p (c m)").bitcast(I32), 0)

        core_bf = keep.tile([P, PASSES, PACK], BF16, name="core_bf")
        nc.scalar.dma_start(out=core_bf[:], in_=core.rearrange("(c p t) -> p c t", c=PASSES, t=PACK))
        w_src = row_weight.rearrange("(j p) -> j p", p=P)
        nc.scalar.dma_start(out=w_rows[:8, :], in_=w_src[:8, :])
        nc.scalar.dma_start(out=w_rows[8:TILES, :], in_=w_src[8:, :])
        core_sb = keep.tile([P, PASSES, PACK], F32, name="core_sb")
        nc.scalar.activation(out=core_sb[:], in_=core_bf[:], func=COPY)

        r_sb = {}
        a_sb = {}
        c_sb = {}

        def load_r(c, g0, g1):
            t = keep.tile([P, PACK, (g1 - g0) * GROUP], BF16, name="r_%d_%d" % (c, g0), align_bytes=64)
            src = r[c * GROUP : (c + 1) * GROUP, g0 * GROUP : g1 * GROUP]
            nc.sync.dma_start(out=t[:], in_=src.rearrange("(p t) n -> p t n", t=PACK))
            for g in range(g0, g1):
                r_sb[(c, g)] = (t, (g - g0) * GROUP)

        def load_a(j0, j1):
            t = keep.tile([P, j1 - j0, N], BF16, name="a_%d" % j0, align_bytes=64)
            nc.sync.dma_start(out=t[:], in_=a[j0 * P : j1 * P, :].rearrange("(j p) n -> p j n", p=P))
            for j in range(j0, j1):
                a_sb[j] = t[:, j - j0, :]

        def load_c(j0, j1):
            t = keep.tile([P, PASSES, (j1 - j0) * P], U32, name="c_%d" % j0, align_bytes=64)
            src = c_words.rearrange("c p m t -> p c (m t)")[:, :, j0 * P * PACK : j1 * P * PACK]
            nc.sync.dma_start(out=t[:].bitcast(I32), in_=src.bitcast(I32))
            for j in range(j0, j1):
                c_sb[j] = t[:, :, (j - j0) * P : (j - j0 + 1) * P]

        load_r(0, 0, 1)
        load_r(0, 1, 2)
        load_r(0, 2, 3)
        load_r(0, 3, 4)
        load_r(1, 0, 2)
        load_r(1, 2, 4)
        for q in range(4):
            nc.sync.dma_start(
                out=c_plane[32 * q : 32 * q + 4, :, :].bitcast(I32),
                in_=c_scales[:, 4 * q : 4 * q + 4, :].rearrange("c r m -> r c m").bitcast(I32),
            )
        load_a(0, 1)
        load_c(0, 4)
        load_a(1, 2)
        load_a(2, 4)
        load_c(4, TILES)
        load_a(4, 8)
        load_a(8, TILES)

        w_f32 = keep.tile([P, P], F32, name="w_f32")
        w_pos = keep.tile([P, TILES], F32, name="w_pos")
        w_neg = keep.tile([P, TILES], F32, name="w_neg")

        def spread_w():
            w_ps = turns.tile([P, 2, 2, P], F32, name="turn")
            nc.tensor.transpose(w_ps[:, 0, 0, :], w_f32[:], ident[:])
            nc.scalar.activation(out=w_pos[:], in_=w_ps[:, 0, 0, :TILES], func=COPY)
            nc.scalar.activation(out=w_neg[:], in_=w_ps[:, 0, 0, :TILES], func=COPY, scale=-1.0)

        ur_codes = keep.tile([P, PASSES * GROUPS, GROUP], U32, name="ur_codes", align_bytes=64)
        ur_plane = keep.tile([P, PASSES * GROUPS, GROUP], U8, name="ur_plane", align_bytes=64)
        y_codes = {}
        for j0, j1 in CODE_STORES:
            t = keep.tile([P, GROUPS, (j1 - j0) * P], U32, name="y_codes_%d" % j0, align_bytes=64)
            for j in range(j0, j1):
                y_codes[j] = (t, j0, j1)
        y_plane = keep.tile([P, M], U8, name="y_plane", align_bytes=64)
        batches = [(0, 1)] + [(j, j + 2) for j in range(1, TILES - 1, 2)] + [(TILES - 1, TILES)]
        batch_of = {j: b for b in batches for j in range(*b)}
        side = {}
        y_sb = {}
        acc = {}
        y_bf = {}
        turned = {}
        y_t = {}

        def scale_r(c, g):
            t, n0 = r_sb[(c, g)]
            for s in range(PACK):
                rows = t[:, s, n0 : n0 + GROUP]
                nc.vector.tensor_scalar(out=rows, in0=rows, scalar1=core_sb[:, c, s : s + 1], scalar2=None, op0=MULT)

        def weave_r(c, g):
            t, n0 = r_sb[(c, g)]
            side[(c, g)] = ring.tile([P, GROUP, PACK], BF16, name="side", bufs=3, align_bytes=64)
            for lo, hi in ((0, WEAVE_SCALAR), (WEAVE_SCALAR, GROUP)):
                dst = side[(c, g)][:, lo:hi, :].rearrange("p (n i) t -> p n t i", i=4)
                src = t[:, :, n0 + lo : n0 + hi].rearrange("p t (n i) -> p n t i", i=4)
                if lo == 0:
                    nc.scalar.copy(out=dst, in_=src)
                else:
                    nc.vector.tensor_copy(out=dst, in_=src)

        def quant_r(c, g):
            nc.vector.quantize_mx(
                out=ur_codes[:, c * GROUPS + g, :].bitcast(E4M3X4),
                scales=ur_plane[:, c * GROUPS + g, :],
                in_=side[(c, g)][:].rearrange("p n t -> p (n t)"),
            )

        def weigh_a(j, g0, g1):
            if j not in y_sb:
                y_sb[j] = ypool.tile([P, N], F32, name="y", align_bytes=64)
            cols = slice(g0 * GROUP, g1 * GROUP)
            nc.scalar.activation(out=y_sb[j][:, cols], in_=a_sb[j][:, cols], func=COPY, scale=w_pos[:, j : j + 1])

        def multiply(j, order):
            for g, c in order:
                if c == 0:
                    acc[(j, g)] = accs.tile([P, GROUP], F32, name="acc")
                nc.tensor.matmul_mx(
                    out=acc[(j, g)][:],
                    lhsT=c_sb[j][:, c, :].bitcast(E5M2X4),
                    lhsT_scale=c_plane[:, c, j * P : (j + 1) * P],
                    rhs=ur_codes[:, c * GROUPS + g, :].bitcast(E4M3X4),
                    rhs_scale=ur_plane[:, c * GROUPS + g, :],
                    start=(c == 0),
                    stop=(c == PASSES - 1),
                )

        by_group = [(g, c) for g in range(GROUPS) for c in range(PASSES)]

        def subtract(j, g0, g1):
            for g in range(g0, g1):
                cols = slice(g * GROUP, (g + 1) * GROUP)
                y = y_sb[j][:, cols]
                if g < POOL_GROUPS and j < TILES - 1:
                    nc.vector.tensor_tensor(out=y, in0=a_sb[j][:, cols], in1=acc[(j, g)][:], op=SUB)
                    nc.gpsimd.tensor_scalar(out=y, in0=y, scalar1=w_pos[:, j : j + 1], scalar2=0.0, op0=MULT, op1=ADD)
                else:
                    nc.vector.scalar_tensor_tensor(out=y, in0=acc[(j, g)][:], scalar=w_neg[:, j : j + 1], in1=y, op0=MULT, op1=ADD)

        def store_y(j, g0, g1):
            cols = slice(g0 * GROUP, g1 * GROUP)
            nc.sync.dma_start(out=out_0[j * P : (j + 1) * P, cols], in_=y_sb[j][:, cols])

        def round_y(j, g0, g1, on_scalar):
            if j not in y_bf:
                y_bf[j] = ring.tile([P, GROUPS, GROUP], BF16, name="y_bf", align_bytes=64)
            if g1 - g0 == 1:
                dst = y_bf[j][:, g0, :].rearrange("m (u h p e) -> m h u p e", h=2, u=2, e=2)
            else:
                dst = y_bf[j][:, g0:g1, :].rearrange("m h (u p e) -> m h u p e", u=2, e=2)
            src = y_sb[j][:, g0 * GROUP : g1 * GROUP].rearrange("m (h p u e) -> m h u p e", h=2, u=2, e=2)
            if on_scalar:
                nc.scalar.copy(out=dst, in_=src)
            else:
                nc.vector.tensor_copy(out=dst, in_=src)

        def turn_y(j, g0, g1):
            words = y_bf[j][:].bitcast(F32)
            turned[(j, g0)] = turns.tile([P, 2, 2, P], F32, name="turn")
            for g in range(g0, g1):
                for u in range(2):
                    nc.tensor.transpose(turned[(j, g0)][:, g - g0, u, :], words[:, g, u * P : (u + 1) * P], ident[:])

        def weave_y(j, g0, g1):
            first = batch_of[j][0]
            if first not in y_t:
                y_t[first] = ring.tile([P, GROUPS, 2 * P, PACK], BF16, name="y_t", align_bytes=64)
            words = y_t[first][:, g0:g1, (j - first) * P : (j - first + 1) * P, :].bitcast(F32)
            src = turned[(j, g0)][:, : g1 - g0, :, :]
            nc.scalar.copy(out=words, in_=src.rearrange("p g u m -> p g m u"))

        def quant_y(batch, g):
            first, end = batch
            t, j0, j1 = y_codes[first]
            nc.vector.quantize_mx(
                out=t[:, g, (first - j0) * P : (end - j0) * P].bitcast(E4M3X4),
                scales=y_plane[4 * g :, first * P : end * P],
                in_=y_t[first][:, g, : (end - first) * P, :].rearrange("p m t -> p (m t)"),
            )
            if g == GROUPS - 1 and end == j1:
                dst = out_1.rearrange("g p m t -> p g (m t)")[:, :, j0 * P * PACK : j1 * P * PACK]
                nc.sync.dma_start(out=dst.bitcast(I32), in_=t[:].bitcast(I32))

        def store_scales(j0, j1, engines):
            for q in range(4):
                engines[q % len(engines)].dma_start(
                    out=out_2[:, 4 * q : 4 * q + 4, j0 * P : j1 * P].bitcast(I32),
                    in_=y_plane[32 * q : 32 * q + 16, j0 * P : j1 * P].bitcast(I32),
                )

        steps = [(c, g) for c in range(PASSES) for g in range(GROUPS)]
        scale_r(0, 0)
        for s in range(len(steps)):
            weave_r(*steps[s])
            if s == PASSES * GROUPS - 3:
                nc.vector.tensor_copy(out=w_f32[:], in_=w_rows[:])
                spread_w()
            if s + 1 < len(steps):
                scale_r(*steps[s + 1])
            if s > 0:
                quant_r(*steps[s - 1])
        quant_r(*steps[-1])
        weigh_a(0, POOL_GROUPS, GROUPS)
        multiply(0, by_group)

        last = TILES - 1
        ready = []

        def quant_next():
            if ready:
                quant_y(*ready.pop(0))

        for j in range(last):
            subtract(j, 0, 1)
            quant_next()
            subtract(j, 1, GROUPS)
            store_y(j, 0, GROUPS)
            multiply(j + 1, by_group)
            if j == 0:
                weigh_a(1, POOL_GROUPS, GROUPS)
            if j + AHEAD < TILES:
                weigh_a(j + AHEAD, POOL_GROUPS, GROUPS)
            else:
                weigh_a(last, 0, POOL_GROUPS)
            if j > 0:
                weave_y(j - 1, 0, 2)
                weave_y(j - 1, 2, 4)
                if batch_of[j - 1][1] == j:
                    ready.extend((batch_of[j - 1], g) for g in range(GROUPS))
            round_y(j, 0, 2, True)
            quant_next()
            round_y(j, 2, 4, False)
            turn_y(j, 0, 2)
            turn_y(j, 2, 4)

        pair, single = batches[-2], batches[-1]
        weave_y(last - 1, 0, 2)
        subtract(last, 0, 1)
        quant_next()
        store_scales(0, pair[0], [nc.sync])
        round_y(last, 0, 1, True)
        subtract(last, 1, 2)
        store_y(last, 0, 2)
        round_y(last, 1, 2, True)
        turn_y(last, 0, 2)
        weave_y(last - 1, 2, 4)
        subtract(last, 2, 4)
        store_y(last, 2, 4)
        for g in range(2, GROUPS):
            quant_y(pair, g - 2)
            round_y(last, g, g + 1, False)
            turn_y(last, g, g + 1)
        weave_y(last, 0, 2)
        weave_y(last, 2, 3)
        weave_y(last, 3, 4)
        for g in range(2):
            quant_y(pair, 2 + g)
            quant_y(single, g)
        quant_y(single, 2)
        quant_y(single, 3)
        store_scales(pair[0], TILES, [nc.sync])
